import numpy as np
import ml_dtypes


def mxq(x, axis, fmt="e4m3"):
    dtype, down = {"e4m3": (ml_dtypes.float8_e4m3fn, 7), "e5m2": (ml_dtypes.float8_e5m2, 14)}[fmt]
    v = np.moveaxis(np.asarray(x, np.float32).astype(ml_dtypes.bfloat16).astype(np.float64), axis, -1)
    blocks = v.reshape(v.shape[:-1] + (-1, 32))
    amax = np.abs(blocks).max(-1, keepdims=True)
    byte = np.maximum(np.where(amax > 0, np.frexp(amax)[1] - 1 + 127, 0) - down, 1)
    scale = np.exp2(byte - 127.0)
    codes = (blocks / scale).astype(np.float32).astype(dtype).astype(np.float64)
    return np.moveaxis((codes * scale).reshape(v.shape), -1, axis)


WIDE = False


def mx_kscale(k):
    if not WIDE:
        return np.ones(k)
    levels = np.array([10, -10, 5, -5, 0])
    if k % 512:
        return np.exp2(np.random.permutation(np.resize(levels, k // 32))).repeat(32)
    a = np.empty((k // 512, 16))
    for p in range(k // 512):
        a[p, :8] = np.random.permutation(np.resize(levels, 8))
        for g in range(8):
            far = levels[np.abs(levels - a[p, g]) >= 10]
            a[p, g + 8] = far[np.random.randint(len(far))]
    return np.exp2(a.ravel()).repeat(32)


def f64(x):
    return np.asarray(x).astype(np.float64)


def striped(idx):
    return np.tile(idx.reshape(-1, 16).T, (8, 1)).astype(np.uint16)


def unstriped(offs):
    return offs[:16].T.reshape(-1).astype(np.int64)


def striped8(idx):
    return np.concatenate([x.reshape(-1, 16).T for x in idx]).astype(np.uint16)


def runs(offs, k):
    lists = np.stack([offs[16 * r : 16 * r + 16].T.reshape(-1) for r in range(8)]).astype(np.int64)
    return lists[np.arange(k) % 512 // 64]


def pack_weight(w):
    k, n = w.shape
    w = f64(np.asarray(w, np.float32).astype(ml_dtypes.bfloat16)).reshape(k // 32, 32, n)
    amax = np.abs(w).max(1)
    byte = np.clip(np.where(amax > 0, np.frexp(amax)[1] - 1 + 127 - 7, 1), 1, 254)
    scaled = (w * np.exp2(127.0 - byte)[:, None, :]).reshape(k, n).astype(np.float32)
    words = np.ascontiguousarray(scaled.reshape(k // 512, 128, 4, n).transpose(0, 1, 3, 2)).astype(ml_dtypes.float8_e4m3fn).view(np.uint8)
    return words, np.ascontiguousarray(byte.astype(np.uint8).reshape(k // 512, 16, n))


def unpack_weight(words, scales):
    g, p, n, _ = words.shape
    vals = np.ascontiguousarray(words).view(ml_dtypes.float8_e4m3fn).astype(np.float64) * np.repeat(np.exp2(scales.astype(np.float64) - 127.0), 8, axis=1)[..., None]
    return vals.transpose(0, 1, 3, 2).reshape(g * 512, n)

def planes(y):
    n, m = y.shape
    v = y.astype(np.float32).astype(ml_dtypes.bfloat16).astype(np.float64).reshape(n // 32, 32, m)
    top = np.abs(v).max(1)
    byte = np.clip(np.where(top > 0, np.frexp(top)[1] - 1 + 127 - 7, 1), 1, 254)
    codes = (v * np.exp2(127.0 - byte)[:, None, :]).reshape(n, m).astype(np.float32).astype(ml_dtypes.float8_e4m3fn).view(np.uint8)
    words = codes.reshape(n // 512, 128, 4, m).transpose(0, 1, 3, 2)
    return np.ascontiguousarray(words), np.ascontiguousarray(byte.astype(np.uint8).reshape(n // 512, 16, m))


K, T, S, N, G, H = 512, 2048, 512, 512, 2048, 512


def setup_inputs():
    n = np.random.standard_normal
    s = mx_kscale(K)[:, None]
    u = mx_kscale(S)
    packed_xT = pack_weight(n((K, T)) * s)
    packed_dT = pack_weight(n((K, G)) / s)
    packed_w1 = pack_weight(n((H, N)) / np.sqrt(H) / u[:, None])
    return {
        "x_words": packed_xT[0],
        "x_scales": packed_xT[1],
        "d_words": packed_dT[0],
        "d_scales": packed_dT[1],
        "gn": (np.random.uniform(0.5, 1.5, (H, 1)) * u[:, None]).astype(np.float32),
        "w1_words": packed_w1[0],
        "w1_scales": packed_w1[1],
        "tau": np.random.uniform(0.5, 1.2, (N, 1)).astype(np.float32),
        "offs": striped(np.random.permutation(T)[:S]),
        "kidx": striped8(np.random.randint(0, G, (8, H))),
        "n1": striped(np.random.randint(0, S, G)),
        "n2": striped(np.random.permutation(S)),
        "n3": striped(np.random.permutation(S)),
    }


def reference(x_words, x_scales, d_words, d_scales, gn, w1_words, w1_scales, tau, offs, kidx, n1, n2, n3):
    d_kidx = unpack_weight(d_words, d_scales)[np.arange(K)[:, None], runs(kidx, K)]
    xq = unpack_weight(x_words, x_scales)[:, unstriped(offs)]
    s = 0.0625 * (d_kidx.T @ xq)
    mb = s[:, unstriped(n1)]
    mx = mb.reshape(H, S, 4).max(axis=2)
    z = f64(gn) * (s - mx)
    h = unpack_weight(w1_words, w1_scales).T @ mxq(z, 0, "e4m3")
    sz = np.abs(h)
    ea = np.exp(-1.0 * (f64(tau) * sz[:, unstriped(n2)]))
    out_0 = (h - h[:, unstriped(n3)]) * ea
    return (out_0,) + planes(out_0)

@@ -1,0 +1,236 @@
+from contextlib import ExitStack
+
+import concourse.mybir as mybir
+
+K, T, S, N, G, H = 512, 2048, 512, 512, 2048, 512
+FLOPS = 2 * K * H * S + 2 * H * N * S
+
+F32 = mybir.dt.float32
+BF16 = mybir.dt.bfloat16
+I32 = mybir.dt.int32
+U32 = mybir.dt.uint32
+U16 = mybir.dt.uint16
+U8 = mybir.dt.uint8
+FP8X4 = mybir.dt.float8_e4m3fn_x4
+ALU = mybir.AluOpType
+ACT = mybir.ActivationFunctionType
+
+P = 128
+PACK = 4
+MEMBERS = 4
+SPARE = 32
+Z_BLOCKS = (128, 128, 128, 64, 64)
+OUT_BLOCKS = (256, 128, 128)
+ABS_EARLY = 384
+VECTOR_N3 = {0: (0, 1, 2, 3)}
+
+
+def spans(widths):
+    starts = [sum(widths[:i]) for i in range(len(widths))]
+    return list(zip(starts, widths))
+
+
+def as_words(dram):
+    return dram[0].rearrange("p n r -> p (n r)").bitcast(I32)
+
+
+def tile_picked_keygmaxdela_none_po_kernel(
+    tc, x_words, x_scales, d_words, d_scales, gn, w1_words, w1_scales, tau, offs, kidx, n1, n2, n3, out_0, out_1, out_2
+):
+    nc = tc.nc
+    with ExitStack() as ctx:
+        lists = ctx.enter_context(tc.tile_pool(name="lists", bufs=1))
+        sb = ctx.enter_context(tc.tile_pool(name="sb", bufs=1))
+        ps = ctx.enter_context(tc.psum_pool(name="ps", bufs=1))
+
+        def keep(shape, dtype, name):
+            return sb.tile(shape, dtype, name=name, align_bytes=64)
+
+        def load_list(dram, name):
+            held = lists.tile([P, dram.shape[1]], U16, name=name)
+            nc.sync.dma_start(held[:], dram)
+            return held
+
+        def load_scale_rows(queue, plane, dram):
+            rows = dram[0].bitcast(I32)
+            for q in range(4):
+                queue.dma_start(plane[:].bitcast(I32)[32 * q : 32 * q + 4, :], rows[4 * q : 4 * q + 4, :])
+
+        def deal(dst, src):
+            nc.vector.tensor_copy(
+                dst[:].rearrange("p (t m) -> p t m", t=PACK), src[:].rearrange("p (m t) -> p t m", t=PACK)
+            )
+
+        d_bytes = keep([P, G], U8, "d_bytes")
+        x_bytes = sb.tile([P, T], U8, name="x_bytes", tag="x_bytes_then_d_picked", align_bytes=64)
+        placed = keep([P, H + S], U8, "placed")
+        for zeroed in (d_bytes, x_bytes, placed):
+            nc.vector.memset(zeroed[:].bitcast(I32), 0)
+        s_rows = [keep([P, S + SPARE], F32, f"s_rows{t}") for t in range(PACK)]
+        for t in range(PACK):
+            nc.vector.memset(s_rows[t][:, S:], 0.0)
+
+        d_table = sb.tile([P, G], U32, name="d_table", tag="d_table_then_w_raw", align_bytes=64)
+        x_table = sb.tile([P, T], U32, name="x_table", tag="x_table_then_w_bytes", align_bytes=64)
+        nc.scalar.dma_start(d_table[:].bitcast(I32), as_words(d_words))
+        kidx_sb = load_list(kidx, "kidx_sb")
+        offs_sb = load_list(offs, "offs_sb")
+        n1_sb = load_list(n1, "n1_sb")
+        n2_sb = load_list(n2, "n2_sb")
+        nc.sync.dma_start(d_bytes[:].bitcast(I32)[0:P:8, :], d_scales[0].bitcast(I32))
+        nc.sync.dma_start(x_bytes[:].bitcast(I32)[0:P:8, :], x_scales[0].bitcast(I32))
+        nc.sync.dma_start(x_table[:].bitcast(I32), as_words(x_words))
+        n3_sb = load_list(n3, "n3_sb")
+        tau_sb = keep([P, PACK], F32, "tau_sb")
+        gn_sb = keep([P, PACK], F32, "gn_sb")
+        nc.gpsimd.dma_start(tau_sb[:], tau.rearrange("(p t) o -> p (t o)", t=PACK))
+        nc.gpsimd.dma_start(gn_sb[:], gn.rearrange("(p t) o -> p (t o)", t=PACK))
+
+        neg_tau = keep([P, PACK], F32, "neg_tau")
+        neg_gn = keep([P, PACK], F32, "neg_gn")
+        nc.scalar.activation(neg_tau[:], tau_sb[:], ACT.Copy, scale=-1.0)
+        nc.scalar.activation(neg_gn[:], gn_sb[:], ACT.Copy, scale=-1.0)
+
+        picked = keep([P, H + S], U8, "picked")
+        nc.vector.tensor_copy(picked[:, :H], d_bytes[:].indirect(kidx_sb[:]))
+        nc.vector.tensor_copy(picked[:, H:], x_bytes[:].indirect(offs_sb[:]))
+        for q in range(4):
+            nc.scalar.dma_start(
+                placed[:].bitcast(I32)[32 * q : 32 * q + 4, :],
+                picked[:].bitcast(I32)[32 * q : 32 * q + 32 : 8, :],
+            )
+        d_picked = sb.tile([P, H], U32, name="d_picked", tag="x_bytes_then_d_picked", align_bytes=64)
+        d_codes = keep([P, H], U32, "d_codes")
+        nc.vector.tensor_copy(d_picked[:], d_table[:].indirect(kidx_sb[:]))
+        deal(d_codes, d_picked)
+        w_raw = sb.tile([P, N], U32, name="w_raw", tag="d_table_then_w_raw", align_bytes=64)
+        nc.sync.dma_start(w_raw[:].bitcast(I32), as_words(w1_words))
+        d_plane = keep([P, H], U8, "d_plane")
+        d_placed = placed[:, :H].rearrange("p (m t) -> p t m", t=PACK)
+
+        half = S // 2
+        x_codes = keep([P, S], U32, "x_codes")
+        first = [ps.tile([P, S], F32, name=f"s_first{c}", tag=f"bank{PACK * c}") for c in range(2)]
+        banks = [ps.tile([P, S], F32, name=f"s_bank{t}", tag=f"bank{t}") for t in range(1, PACK)]
+
+        def score(acc, t, cols):
+            nc.tensor.matmul_mx(
+                out=acc,
+                lhsT=d_codes[:, t * P : (t + 1) * P].bitcast(FP8X4),
+                lhsT_scale=d_plane[:, t * P : (t + 1) * P],
+                rhs=x_codes[:, cols].bitcast(FP8X4),
+                rhs_scale=placed[:, H:][:, cols],
+                start=True,
+                stop=True,
+            )
+
+        for c in range(2):
+            cols = slice(c * half, (c + 1) * half)
+            entries = offs_sb[:, c * half // 16 : (c + 1) * half // 16]
+            nc.vector.tensor_copy(x_codes[:, cols], x_table[:].indirect(entries))
+        nc.vector.tensor_copy(d_plane[:, :P], d_placed[:, 0, :])
+        nc.vector.tensor_copy(d_plane[:, P:].rearrange("p (t m) -> p t m", m=P), d_placed[:, 1:, :])
+        for c in range(2):
+            cols = slice(c * half, (c + 1) * half)
+            score(first[c][:, :half], 0, cols)
+            nc.scalar.activation(s_rows[0][:, cols], first[c][:, :half], ACT.Copy, scale=0.0625)
+        for t in range(1, PACK):
+            score(banks[t - 1][:], t, slice(0, S))
+            nc.vector.tensor_scalar(s_rows[t][:, :S], banks[t - 1][:], 0.0625, None, ALU.mult)
+
+        w_bytes = sb.tile([P, N], U8, name="w_bytes", tag="x_table_then_w_bytes", align_bytes=64)
+        nc.vector.memset(w_bytes[:].bitcast(I32), 0)
+        load_scale_rows(nc.sync, w_bytes, w1_scales)
+        w_codes = keep([P, N], U32, "w_codes")
+        w_plane = keep([P, N], U8, "w_plane")
+
+        s_gn = keep([P, PACK, S], F32, "s_gn")
+        for t in range(PACK):
+            nc.vector.tensor_scalar(s_gn[:, t, :], s_rows[t][:, :S], gn_sb[:, t : t + 1], None, ALU.mult)
+
+        deal(w_codes, w_raw)
+        deal(w_plane, w_bytes)
+
+        h_rows = keep([P, PACK, S], F32, "h_rows")
+        h_early = [ps.tile([P, S], F32, name=f"h_early{t}", tag=f"bank{t}") for t in range(PACK)]
+        for b, (j0, width) in enumerate(spans(Z_BLOCKS)):
+            cols = slice(j0, j0 + width)
+            members = keep([P, PACK, width * MEMBERS], F32, f"members{b}")
+            pairs = keep([P, PACK, width, 2], F32, f"pairs{b}")
+            top = keep([P, PACK, width], F32, f"top{b}")
+            z32 = keep([P, PACK, width], F32, f"z32_{b}")
+            entries = n1_sb[:, j0 * MEMBERS // 16 : (j0 + width) * MEMBERS // 16]
+            for t in range(PACK):
+                nc.scalar.activation(members[:, t, :], s_rows[t][:].indirect(entries), ACT.Copy)
+                grouped = members[:, t, :].rearrange("p (j e) -> p j e", e=MEMBERS)
+                nc.vector.tensor_tensor(pairs[:, t, :, :], grouped[:, :, 0:2], grouped[:, :, 2:4], ALU.max)
+            nc.vector.tensor_tensor(top[:], pairs[:, :, :, 0], pairs[:, :, :, 1], ALU.max)
+            for t in range(PACK):
+                nc.vector.scalar_tensor_tensor(
+                    z32[:, t, :], top[:, t, :], neg_gn[:, t : t + 1], s_gn[:, t, cols], ALU.mult, ALU.add
+                )
+            z16 = keep([P, width * PACK], BF16, f"z16_{b}")
+            nc.vector.tensor_copy(
+                z16[:].rearrange("p (c i t) -> p c t i", i=4, t=PACK), z32[:].rearrange("p t (c i) -> p c t i", i=4)
+            )
+            z_codes = keep([P, width], U32, f"z_codes{b}")
+            z_plane = keep([P, width], U8, f"z_plane{b}")
+            nc.vector.quantize_mx(out=z_codes[:].bitcast(FP8X4), scales=z_plane[:], in_=z16[:])
+            late = j0 >= ABS_EARLY
+            if late:
+                h_late = ps.tile([P, PACK, width], F32, name=f"h_late{b}", tag=f"late{b}")
+            for t in range(PACK):
+                nc.tensor.matmul_mx(
+                    out=h_late[:, t, :] if late else h_early[t][:, cols],
+                    lhsT=w_codes[:, t * P : (t + 1) * P].bitcast(FP8X4),
+                    lhsT_scale=w_plane[:, t * P : (t + 1) * P],
+                    rhs=z_codes[:].bitcast(FP8X4),
+                    rhs_scale=z_plane[:],
+                    start=True,
+                    stop=True,
+                )
+            if late:
+                nc.vector.tensor_copy(h_rows[:, :, cols], h_late[:])
+
+        sz_rows = [keep([P, S], F32, f"sz_rows{t}") for t in range(PACK)]
+        for t in range(PACK):
+            nc.scalar.activation(h_rows[:, t, :ABS_EARLY], h_early[t][:, :ABS_EARLY], ACT.Copy)
+        for t in range(PACK):
+            nc.scalar.activation(sz_rows[t][:, :ABS_EARLY], h_early[t][:, :ABS_EARLY], ACT.Abs)
+        for t in range(PACK):
+            nc.scalar.activation(sz_rows[t][:, ABS_EARLY:], h_rows[:, t, ABS_EARLY:], ACT.Abs)
+
+        out_rows = out_0.rearrange("(p t) j -> p t j", t=PACK)
+        out_words = as_words(out_1)
+        y_plane = keep([P, S], U8, "y_plane")
+        for b, (j0, width) in enumerate(spans(OUT_BLOCKS)):
+            cols = slice(j0, j0 + width)
+            entries = slice(j0 // 16, (j0 + width) // 16)
+            h_other = keep([P, PACK, width], F32, f"h_other{b}")
+            ea = keep([P, PACK, width], F32, f"ea{b}")
+            for t in range(PACK):
+                window = h_rows[:, t, :].indirect(n3_sb[:, entries])
+                if t in VECTOR_N3.get(b, ()):
+                    nc.vector.tensor_copy(h_other[:, t, :], window)
+                else:
+                    nc.scalar.activation(h_other[:, t, :], window, ACT.Copy)
+            for t in range(PACK):
+                nc.scalar.activation(
+                    ea[:, t, :], sz_rows[t][:].indirect(n2_sb[:, entries]), ACT.Exp, scale=neg_tau[:, t : t + 1]
+                )
+            delta = keep([P, PACK, width], F32, f"delta{b}")
+            y32 = keep([P, PACK, width], F32, f"y32_{b}")
+            nc.vector.tensor_tensor(delta[:], h_rows[:, :, cols], h_other[:], ALU.subtract)
+            nc.vector.tensor_tensor(y32[:], delta[:], ea[:], ALU.mult)
+            nc.sync.dma_start(out_rows[:, :, cols], y32[:])
+            y16 = keep([P, width * PACK], BF16, f"y16_{b}")
+            nc.vector.tensor_copy(
+                y16[:].rearrange("p (c i t) -> p c t i", i=4, t=PACK), y32[:].rearrange("p t (c i) -> p c t i", i=4)
+            )
+            y_codes = keep([P, width], U32, f"y_codes{b}")
+            nc.vector.quantize_mx(out=y_codes[:].bitcast(FP8X4), scales=y_plane[:, cols], in_=y16[:])
+            nc.sync.dma_start(out_words[:, cols], y_codes[:].bitcast(I32))
+        scale_rows = out_2[0].bitcast(I32)
+        for q in range(4):
+            queue = nc.scalar if q % 2 == 0 else nc.sync
+            queue.dma_start(scale_rows[4 * q : 4 * q + 4, :], y_plane[:].bitcast(I32)[32 * q : 32 * q + 4, :])

@@ -14,6 +14,7 @@ U8 = mybir.dt.uint8
 FP8X4 = mybir.dt.float8_e4m3fn_x4
 ALU = mybir.AluOpType
 ACT = mybir.ActivationFunctionType
+AX = mybir.AxisListType
 
 P = 128
 PACK = 4
@@ -22,7 +23,7 @@ SPARE = 32
 Z_BLOCKS = (128, 128, 128, 64, 64)
 OUT_BLOCKS = (256, 128, 128)
 ABS_EARLY = 384
-VECTOR_N3 = {0: (0, 1, 2, 3)}
+SCALAR_H_BLOCK = 2
 
 
 def spans(widths):
@@ -56,9 +57,16 @@ def tile_picked_keygmaxdela_none_po_kernel(
             for q in range(4):
                 queue.dma_start(plane[:].bitcast(I32)[32 * q : 32 * q + 4, :], rows[4 * q : 4 * q + 4, :])
 
-        def deal(dst, src):
+        def deal(dst, src, run):
             nc.vector.tensor_copy(
-                dst[:].rearrange("p (t m) -> p t m", t=PACK), src[:].rearrange("p (m t) -> p t m", t=PACK)
+                dst[:].rearrange("p (t c i) -> p c t i", t=PACK, i=run),
+                src[:].rearrange("p (c i t) -> p c t i", t=PACK, i=run),
+            )
+
+        def interleave(dst16, src32):
+            nc.vector.tensor_copy(
+                dst16[:].rearrange("p (c i t) -> p c t i", i=4, t=PACK),
+                src32[:].rearrange("p t (c i) -> p c t i", i=4),
             )
 
         d_bytes = keep([P, G], U8, "d_bytes")
@@ -72,24 +80,29 @@ def tile_picked_keygmaxdela_none_po_kernel(
 
         d_table = sb.tile([P, G], U32, name="d_table", tag="d_table_then_w_raw", align_bytes=64)
         x_table = sb.tile([P, T], U32, name="x_table", tag="x_table_then_w_bytes", align_bytes=64)
-        nc.scalar.dma_start(d_table[:].bitcast(I32), as_words(d_words))
+
+        def load_dictionary(c0, c1):
+            nc.sync.dma_start(d_table[:, c0:c1].bitcast(I32), as_words(d_words)[:, c0:c1])
+
         kidx_sb = load_list(kidx, "kidx_sb")
         offs_sb = load_list(offs, "offs_sb")
+        load_dictionary(0, G // 4)
         n1_sb = load_list(n1, "n1_sb")
-        n2_sb = load_list(n2, "n2_sb")
         nc.sync.dma_start(d_bytes[:].bitcast(I32)[0:P:8, :], d_scales[0].bitcast(I32))
         nc.sync.dma_start(x_bytes[:].bitcast(I32)[0:P:8, :], x_scales[0].bitcast(I32))
+        load_dictionary(G // 4, G)
         nc.sync.dma_start(x_table[:].bitcast(I32), as_words(x_words))
+        n2_sb = load_list(n2, "n2_sb")
         n3_sb = load_list(n3, "n3_sb")
         tau_sb = keep([P, PACK], F32, "tau_sb")
         gn_sb = keep([P, PACK], F32, "gn_sb")
-        nc.gpsimd.dma_start(tau_sb[:], tau.rearrange("(p t) o -> p (t o)", t=PACK))
         nc.gpsimd.dma_start(gn_sb[:], gn.rearrange("(p t) o -> p (t o)", t=PACK))
+        nc.gpsimd.dma_start(tau_sb[:], tau.rearrange("(p t) o -> p (t o)", t=PACK))
 
         neg_tau = keep([P, PACK], F32, "neg_tau")
         neg_gn = keep([P, PACK], F32, "neg_gn")
-        nc.scalar.activation(neg_tau[:], tau_sb[:], ACT.Copy, scale=-1.0)
-        nc.scalar.activation(neg_gn[:], gn_sb[:], ACT.Copy, scale=-1.0)
+        nc.gpsimd.tensor_scalar(neg_gn[:], gn_sb[:], -1.0, 0.0, ALU.mult, ALU.add)
+        nc.gpsimd.tensor_scalar(neg_tau[:], tau_sb[:], -1.0, 0.0, ALU.mult, ALU.add)
 
         picked = keep([P, H + S], U8, "picked")
         nc.vector.tensor_copy(picked[:, :H], d_bytes[:].indirect(kidx_sb[:]))
@@ -100,12 +113,12 @@ def tile_picked_keygmaxdela_none_po_kernel(
                 picked[:].bitcast(I32)[32 * q : 32 * q + 32 : 8, :],
             )
         d_picked = sb.tile([P, H], U32, name="d_picked", tag="x_bytes_then_d_picked", align_bytes=64)
-        d_codes = keep([P, H], U32, "d_codes")
+        d_codes = sb.tile([P, H], U32, name="d_codes", tag="stationary_codes", align_bytes=64)
         nc.vector.tensor_copy(d_picked[:], d_table[:].indirect(kidx_sb[:]))
-        deal(d_codes, d_picked)
+        deal(d_codes, d_picked, 4)
         w_raw = sb.tile([P, N], U32, name="w_raw", tag="d_table_then_w_raw", align_bytes=64)
         nc.sync.dma_start(w_raw[:].bitcast(I32), as_words(w1_words))
-        d_plane = keep([P, H], U8, "d_plane")
+        d_plane = sb.tile([P, H], U8, name="d_plane", tag="stationary_plane", align_bytes=64)
         d_placed = placed[:, :H].rearrange("p (m t) -> p t m", t=PACK)
 
         half = S // 2
@@ -141,47 +154,57 @@ def tile_picked_keygmaxdela_none_po_kernel(
         w_bytes = sb.tile([P, N], U8, name="w_bytes", tag="x_table_then_w_bytes", align_bytes=64)
         nc.vector.memset(w_bytes[:].bitcast(I32), 0)
         load_scale_rows(nc.sync, w_bytes, w1_scales)
-        w_codes = keep([P, N], U32, "w_codes")
-        w_plane = keep([P, N], U8, "w_plane")
+        w_codes = sb.tile([P, N], U32, name="w_codes", tag="stationary_codes", align_bytes=64)
+        w_plane = sb.tile([P, N], U8, name="w_plane", tag="stationary_plane", align_bytes=64)
 
         s_gn = keep([P, PACK, S], F32, "s_gn")
         for t in range(PACK):
             nc.vector.tensor_scalar(s_gn[:, t, :], s_rows[t][:, :S], gn_sb[:, t : t + 1], None, ALU.mult)
 
-        deal(w_codes, w_raw)
-        deal(w_plane, w_bytes)
+        deal(w_codes, w_raw, 4)
+        deal(w_plane, w_bytes, 16)
 
         h_rows = keep([P, PACK, S], F32, "h_rows")
-        h_early = [ps.tile([P, S], F32, name=f"h_early{t}", tag=f"bank{t}") for t in range(PACK)]
-        for b, (j0, width) in enumerate(spans(Z_BLOCKS)):
+        sz_rows = [keep([P, S], F32, f"sz_rows{t}") for t in range(PACK)]
+        blocks = spans(Z_BLOCKS)
+        last = len(blocks) - 1
+        h_banks = []
+        for b, (j0, width) in enumerate(blocks):
             cols = slice(j0, j0 + width)
             members = keep([P, PACK, width * MEMBERS], F32, f"members{b}")
-            pairs = keep([P, PACK, width, 2], F32, f"pairs{b}")
             top = keep([P, PACK, width], F32, f"top{b}")
-            z32 = keep([P, PACK, width], F32, f"z32_{b}")
-            entries = n1_sb[:, j0 * MEMBERS // 16 : (j0 + width) * MEMBERS // 16]
-            for t in range(PACK):
-                nc.scalar.activation(members[:, t, :], s_rows[t][:].indirect(entries), ACT.Copy)
-                grouped = members[:, t, :].rearrange("p (j e) -> p j e", e=MEMBERS)
-                nc.vector.tensor_tensor(pairs[:, t, :, :], grouped[:, :, 0:2], grouped[:, :, 2:4], ALU.max)
-            nc.vector.tensor_tensor(top[:], pairs[:, :, :, 0], pairs[:, :, :, 1], ALU.max)
-            for t in range(PACK):
-                nc.vector.scalar_tensor_tensor(
-                    z32[:, t, :], top[:, t, :], neg_gn[:, t : t + 1], s_gn[:, t, cols], ALU.mult, ALU.add
-                )
             z16 = keep([P, width * PACK], BF16, f"z16_{b}")
-            nc.vector.tensor_copy(
-                z16[:].rearrange("p (c i t) -> p c t i", i=4, t=PACK), z32[:].rearrange("p t (c i) -> p c t i", i=4)
-            )
+            entries = n1_sb[:, j0 * MEMBERS // 16 : (j0 + width) * MEMBERS // 16]
+
+            def weigh(z_row, t):
+                nc.vector.scalar_tensor_tensor(
+                    z_row, top[:, t, :], neg_gn[:, t : t + 1], s_gn[:, t, cols], ALU.mult, ALU.add
+                )
+
+            if b < last:
+                pairs = keep([P, PACK, width, 2], F32, f"pairs{b}")
+                z32 = keep([P, PACK, width], F32, f"z32_{b}")
+                for t in range(PACK):
+                    nc.scalar.activation(members[:, t, :], s_rows[t][:].indirect(entries), ACT.Copy)
+                    grouped = members[:, t, :].rearrange("p (j e) -> p j e", e=MEMBERS)
+                    nc.vector.tensor_tensor(pairs[:, t, :, :], grouped[:, :, 0:2], grouped[:, :, 2:4], ALU.max)
+                nc.vector.tensor_tensor(top[:], pairs[:, :, :, 0], pairs[:, :, :, 1], ALU.max)
+                for t in range(PACK):
+                    weigh(z32[:, t, :], t)
+                interleave(z16, z32)
+            else:
+                for t in range(PACK):
+                    nc.scalar.activation(members[:, t, :], s_rows[t][:].indirect(entries), ACT.Copy)
+                    grouped = members[:, t, :].rearrange("p (j e) -> p j e", e=MEMBERS)
+                    nc.vector.tensor_reduce(top[:, t, :], grouped, AX.X, ALU.max)
+                    weigh(z16[:].rearrange("p (j t) -> p t j", t=PACK)[:, t, :], t)
             z_codes = keep([P, width], U32, f"z_codes{b}")
             z_plane = keep([P, width], U8, f"z_plane{b}")
             nc.vector.quantize_mx(out=z_codes[:].bitcast(FP8X4), scales=z_plane[:], in_=z16[:])
-            late = j0 >= ABS_EARLY
-            if late:
-                h_late = ps.tile([P, PACK, width], F32, name=f"h_late{b}", tag=f"late{b}")
-            for t in range(PACK):
+
+            def values(acc, t):
                 nc.tensor.matmul_mx(
-                    out=h_late[:, t, :] if late else h_early[t][:, cols],
+                    out=acc,
                     lhsT=w_codes[:, t * P : (t + 1) * P].bitcast(FP8X4),
                     lhsT_scale=w_plane[:, t * P : (t + 1) * P],
                     rhs=z_codes[:].bitcast(FP8X4),
@@ -189,16 +212,24 @@ def tile_picked_keygmaxdela_none_po_kernel(
                     start=True,
                     stop=True,
                 )
-            if late:
-                nc.vector.tensor_copy(h_rows[:, :, cols], h_late[:])
 
-        sz_rows = [keep([P, S], F32, f"sz_rows{t}") for t in range(PACK)]
-        for t in range(PACK):
-            nc.scalar.activation(h_rows[:, t, :ABS_EARLY], h_early[t][:, :ABS_EARLY], ACT.Copy)
-        for t in range(PACK):
-            nc.scalar.activation(sz_rows[t][:, :ABS_EARLY], h_early[t][:, :ABS_EARLY], ACT.Abs)
-        for t in range(PACK):
-            nc.scalar.activation(sz_rows[t][:, ABS_EARLY:], h_rows[:, t, ABS_EARLY:], ACT.Abs)
+            if b < last:
+                h_banks.append(ps.tile([P, PACK, width], F32, name=f"h_bank{b}", tag=f"bank{b}"))
+                for t in range(PACK):
+                    values(h_banks[b][:, t, :], t)
+                if b != SCALAR_H_BLOCK:
+                    nc.vector.tensor_copy(h_rows[:, :, cols], h_banks[b][:])
+            else:
+                h_last = [ps.tile([P, width], F32, name=f"h_last{t}", tag=f"bank{PACK + t}") for t in range(PACK)]
+                for t in range(PACK):
+                    values(h_last[t][:], t)
+
+        j0, width = blocks[SCALAR_H_BLOCK]
+        nc.scalar.activation(h_rows[:, :, j0 : j0 + width], h_banks[SCALAR_H_BLOCK][:], ACT.Copy)
+        for cols in (slice(0, ABS_EARLY), slice(ABS_EARLY, blocks[last][0])):
+            for t in range(PACK):
+                nc.scalar.activation(sz_rows[t][:, cols], h_rows[:, t, cols], ACT.Abs)
+        last_cols = slice(blocks[last][0], S)
 
         out_rows = out_0.rearrange("(p t) j -> p t j", t=PACK)
         out_words = as_words(out_1)
@@ -208,25 +239,30 @@ def tile_picked_keygmaxdela_none_po_kernel(
             entries = slice(j0 // 16, (j0 + width) // 16)
             h_other = keep([P, PACK, width], F32, f"h_other{b}")
             ea = keep([P, PACK, width], F32, f"ea{b}")
-            for t in range(PACK):
-                window = h_rows[:, t, :].indirect(n3_sb[:, entries])
-                if t in VECTOR_N3.get(b, ()):
-                    nc.vector.tensor_copy(h_other[:, t, :], window)
-                else:
-                    nc.scalar.activation(h_other[:, t, :], window, ACT.Copy)
-            for t in range(PACK):
+
+            def gate(t):
                 nc.scalar.activation(
                     ea[:, t, :], sz_rows[t][:].indirect(n2_sb[:, entries]), ACT.Exp, scale=neg_tau[:, t : t + 1]
                 )
+
+            if b == 0:
+                for t in range(PACK):
+                    nc.scalar.activation(sz_rows[t][:, last_cols], h_last[t][:], ACT.Abs)
+                    nc.vector.tensor_copy(h_rows[:, t, last_cols], h_last[t][:])
+                    gate(t)
+                    nc.vector.tensor_copy(h_other[:, t, :], h_rows[:, t, :].indirect(n3_sb[:, entries]))
+            else:
+                for t in range(PACK):
+                    nc.scalar.activation(h_other[:, t, :], h_rows[:, t, :].indirect(n3_sb[:, entries]), ACT.Copy)
+                for t in range(PACK):
+                    gate(t)
             delta = keep([P, PACK, width], F32, f"delta{b}")
             y32 = keep([P, PACK, width], F32, f"y32_{b}")
             nc.vector.tensor_tensor(delta[:], h_rows[:, :, cols], h_other[:], ALU.subtract)
             nc.vector.tensor_tensor(y32[:], delta[:], ea[:], ALU.mult)
             nc.sync.dma_start(out_rows[:, :, cols], y32[:])
             y16 = keep([P, width * PACK], BF16, f"y16_{b}")
-            nc.vector.tensor_copy(
-                y16[:].rearrange("p (c i t) -> p c t i", i=4, t=PACK), y32[:].rearrange("p t (c i) -> p c t i", i=4)
-            )
+            interleave(y16, y32)
             y_codes = keep([P, width], U32, f"y_codes{b}")
             nc.vector.quantize_mx(out=y_codes[:].bitcast(FP8X4), scales=y_plane[:, cols], in_=y16[:])
             nc.sync.dma_start(out_words[:, cols], y_codes[:].bitcast(I32))

@@ -245,28 +245,35 @@ def tile_picked_keygmaxdela_none_po_kernel(
                     ea[:, t, :], sz_rows[t][:].indirect(n2_sb[:, entries]), ACT.Exp, scale=neg_tau[:, t : t + 1]
                 )
 
+            delta = keep([P, PACK, width], F32, f"delta{b}")
             if b == 0:
                 for t in range(PACK):
                     nc.scalar.activation(sz_rows[t][:, last_cols], h_last[t][:], ACT.Abs)
                     nc.vector.tensor_copy(h_rows[:, t, last_cols], h_last[t][:])
                     gate(t)
                     nc.vector.tensor_copy(h_other[:, t, :], h_rows[:, t, :].indirect(n3_sb[:, entries]))
+                    nc.gpsimd.tensor_tensor(delta[:, t, :], h_rows[:, t, cols], h_other[:, t, :], ALU.subtract)
             else:
                 for t in range(PACK):
-                    nc.scalar.activation(h_other[:, t, :], h_rows[:, t, :].indirect(n3_sb[:, entries]), ACT.Copy)
+                    window = h_rows[:, t, :].indirect(n3_sb[:, entries])
+                    if b == 1 and t < 2:
+                        nc.vector.tensor_copy(h_other[:, t, :], window)
+                    else:
+                        nc.scalar.activation(h_other[:, t, :], window, ACT.Copy)
                 for t in range(PACK):
                     gate(t)
-            delta = keep([P, PACK, width], F32, f"delta{b}")
             y32 = keep([P, PACK, width], F32, f"y32_{b}")
-            nc.vector.tensor_tensor(delta[:], h_rows[:, :, cols], h_other[:], ALU.subtract)
-            nc.vector.tensor_tensor(y32[:], delta[:], ea[:], ALU.mult)
+            if b > 0:
+                nc.vector.tensor_tensor(delta[:], h_rows[:, :, cols], h_other[:], ALU.subtract)
+            for rows in (slice(0, PACK),) if b == 1 else (slice(0, 2), slice(2, PACK)):
+                nc.vector.tensor_tensor(y32[:, rows, :], delta[:, rows, :], ea[:, rows, :], ALU.mult)
             nc.sync.dma_start(out_rows[:, :, cols], y32[:])
             y16 = keep([P, width * PACK], BF16, f"y16_{b}")
             interleave(y16, y32)
             y_codes = keep([P, width], U32, f"y_codes{b}")
             nc.vector.quantize_mx(out=y_codes[:].bitcast(FP8X4), scales=y_plane[:, cols], in_=y16[:])
-            nc.sync.dma_start(out_words[:, cols], y_codes[:].bitcast(I32))
+            nc.scalar.dma_start(out_words[:, cols], y_codes[:].bitcast(I32))
         scale_rows = out_2[0].bitcast(I32)
         for q in range(4):
-            queue = nc.scalar if q % 2 == 0 else nc.sync
+            queue = nc.sync if q % 2 == 0 else nc.scalar
             queue.dma_start(scale_rows[4 * q : 4 * q + 4, :], y_plane[:].bitcast(I32)[32 * q : 32 * q + 4, :])

from contextlib import ExitStack

import concourse.mybir as mybir

K, T, S, N, G, H = 512, 2048, 512, 512, 2048, 512
FLOPS = 2 * K * H * S + 2 * H * N * S

F32 = mybir.dt.float32
BF16 = mybir.dt.bfloat16
I32 = mybir.dt.int32
U32 = mybir.dt.uint32
U16 = mybir.dt.uint16
U8 = mybir.dt.uint8
FP8X4 = mybir.dt.float8_e4m3fn_x4
ALU = mybir.AluOpType
ACT = mybir.ActivationFunctionType
AX = mybir.AxisListType

P = 128
PACK = 4
MEMBERS = 4
SPARE = 32
Z_BLOCKS = (128, 128, 128, 64, 64)
OUT_BLOCKS = (256, 128, 128)
ABS_EARLY = 384
SCALAR_H_BLOCK = 2


def spans(widths):
    starts = [sum(widths[:i]) for i in range(len(widths))]
    return list(zip(starts, widths))


def as_words(dram):
    return dram[0].rearrange("p n r -> p (n r)").bitcast(I32)


def tile_picked_keygmaxdela_none_po_kernel(
    tc, x_words, x_scales, d_words, d_scales, gn, w1_words, w1_scales, tau, offs, kidx, n1, n2, n3, out_0, out_1, out_2
):
    nc = tc.nc
    with ExitStack() as ctx:
        lists = ctx.enter_context(tc.tile_pool(name="lists", bufs=1))
        sb = ctx.enter_context(tc.tile_pool(name="sb", bufs=1))
        ps = ctx.enter_context(tc.psum_pool(name="ps", bufs=1))

        def keep(shape, dtype, name):
            return sb.tile(shape, dtype, name=name, align_bytes=64)

        def load_list(dram, name):
            held = lists.tile([P, dram.shape[1]], U16, name=name)
            nc.sync.dma_start(held[:], dram)
            return held

        def load_scale_rows(queue, plane, dram):
            rows = dram[0].bitcast(I32)
            for q in range(4):
                queue.dma_start(plane[:].bitcast(I32)[32 * q : 32 * q + 4, :], rows[4 * q : 4 * q + 4, :])

        def deal(dst, src, run):
            nc.vector.tensor_copy(
                dst[:].rearrange("p (t c i) -> p c t i", t=PACK, i=run),
                src[:].rearrange("p (c i t) -> p c t i", t=PACK, i=run),
            )

        def interleave(dst16, src32):
            nc.vector.tensor_copy(
                dst16[:].rearrange("p (c i t) -> p c t i", i=4, t=PACK),
                src32[:].rearrange("p t (c i) -> p c t i", i=4),
            )

        d_bytes = keep([P, G], U8, "d_bytes")
        x_bytes = sb.tile([P, T], U8, name="x_bytes", tag="x_bytes_then_d_picked", align_bytes=64)
        placed = keep([P, H + S], U8, "placed")
        for zeroed in (d_bytes, x_bytes, placed):
            nc.vector.memset(zeroed[:].bitcast(I32), 0)
        s_rows = [keep([P, S + SPARE], F32, f"s_rows{t}") for t in range(PACK)]
        for t in range(PACK):
            nc.vector.memset(s_rows[t][:, S:], 0.0)

        d_table = sb.tile([P, G], U32, name="d_table", tag="d_table_then_w_raw", align_bytes=64)
        x_table = sb.tile([P, T], U32, name="x_table", tag="x_table_then_w_bytes", align_bytes=64)

        def load_dictionary(c0, c1):
            nc.sync.dma_start(d_table[:, c0:c1].bitcast(I32), as_words(d_words)[:, c0:c1])

        kidx_sb = load_list(kidx, "kidx_sb")
        offs_sb = load_list(offs, "offs_sb")
        load_dictionary(0, G // 4)
        n1_sb = load_list(n1, "n1_sb")
        nc.sync.dma_start(d_bytes[:].bitcast(I32)[0:P:8, :], d_scales[0].bitcast(I32))
        nc.sync.dma_start(x_bytes[:].bitcast(I32)[0:P:8, :], x_scales[0].bitcast(I32))
        load_dictionary(G // 4, G)
        nc.sync.dma_start(x_table[:].bitcast(I32), as_words(x_words))
        n2_sb = load_list(n2, "n2_sb")
        n3_sb = load_list(n3, "n3_sb")
        tau_sb = keep([P, PACK], F32, "tau_sb")
        gn_sb = keep([P, PACK], F32, "gn_sb")
        nc.gpsimd.dma_start(gn_sb[:], gn.rearrange("(p t) o -> p (t o)", t=PACK))
        nc.gpsimd.dma_start(tau_sb[:], tau.rearrange("(p t) o -> p (t o)", t=PACK))

        neg_tau = keep([P, PACK], F32, "neg_tau")
        neg_gn = keep([P, PACK], F32, "neg_gn")
        nc.gpsimd.tensor_scalar(neg_gn[:], gn_sb[:], -1.0, 0.0, ALU.mult, ALU.add)
        nc.gpsimd.tensor_scalar(neg_tau[:], tau_sb[:], -1.0, 0.0, ALU.mult, ALU.add)

        picked = keep([P, H + S], U8, "picked")
        nc.vector.tensor_copy(picked[:, :H], d_bytes[:].indirect(kidx_sb[:]))
        nc.vector.tensor_copy(picked[:, H:], x_bytes[:].indirect(offs_sb[:]))
        for q in range(4):
            nc.scalar.dma_start(
                placed[:].bitcast(I32)[32 * q : 32 * q + 4, :],
                picked[:].bitcast(I32)[32 * q : 32 * q + 32 : 8, :],
            )
        d_picked = sb.tile([P, H], U32, name="d_picked", tag="x_bytes_then_d_picked", align_bytes=64)
        d_codes = sb.tile([P, H], U32, name="d_codes", tag="stationary_codes", align_bytes=64)
        nc.vector.tensor_copy(d_picked[:], d_table[:].indirect(kidx_sb[:]))
        deal(d_codes, d_picked, 4)
        w_raw = sb.tile([P, N], U32, name="w_raw", tag="d_table_then_w_raw", align_bytes=64)
        nc.sync.dma_start(w_raw[:].bitcast(I32), as_words(w1_words))
        d_plane = sb.tile([P, H], U8, name="d_plane", tag="stationary_plane", align_bytes=64)
        d_placed = placed[:, :H].rearrange("p (m t) -> p t m", t=PACK)

        half = S // 2
        x_codes = keep([P, S], U32, "x_codes")
        first = [ps.tile([P, S], F32, name=f"s_first{c}", tag=f"bank{PACK * c}") for c in range(2)]
        banks = [ps.tile([P, S], F32, name=f"s_bank{t}", tag=f"bank{t}") for t in range(1, PACK)]

        def score(acc, t, cols):
            nc.tensor.matmul_mx(
                out=acc,
                lhsT=d_codes[:, t * P : (t + 1) * P].bitcast(FP8X4),
                lhsT_scale=d_plane[:, t * P : (t + 1) * P],
                rhs=x_codes[:, cols].bitcast(FP8X4),
                rhs_scale=placed[:, H:][:, cols],
                start=True,
                stop=True,
            )

        for c in range(2):
            cols = slice(c * half, (c + 1) * half)
            entries = offs_sb[:, c * half // 16 : (c + 1) * half // 16]
            nc.vector.tensor_copy(x_codes[:, cols], x_table[:].indirect(entries))
        nc.vector.tensor_copy(d_plane[:, :P], d_placed[:, 0, :])
        nc.vector.tensor_copy(d_plane[:, P:].rearrange("p (t m) -> p t m", m=P), d_placed[:, 1:, :])
        for c in range(2):
            cols = slice(c * half, (c + 1) * half)
            score(first[c][:, :half], 0, cols)
            nc.scalar.activation(s_rows[0][:, cols], first[c][:, :half], ACT.Copy, scale=0.0625)
        for t in range(1, PACK):
            score(banks[t - 1][:], t, slice(0, S))
            nc.vector.tensor_scalar(s_rows[t][:, :S], banks[t - 1][:], 0.0625, None, ALU.mult)

        w_bytes = sb.tile([P, N], U8, name="w_bytes", tag="x_table_then_w_bytes", align_bytes=64)
        nc.vector.memset(w_bytes[:].bitcast(I32), 0)
        load_scale_rows(nc.sync, w_bytes, w1_scales)
        w_codes = sb.tile([P, N], U32, name="w_codes", tag="stationary_codes", align_bytes=64)
        w_plane = sb.tile([P, N], U8, name="w_plane", tag="stationary_plane", align_bytes=64)

        s_gn = keep([P, PACK, S], F32, "s_gn")
        for t in range(PACK):
            nc.vector.tensor_scalar(s_gn[:, t, :], s_rows[t][:, :S], gn_sb[:, t : t + 1], None, ALU.mult)

        deal(w_codes, w_raw, 4)
        deal(w_plane, w_bytes, 16)

        h_rows = keep([P, PACK, S], F32, "h_rows")
        sz_rows = [keep([P, S], F32, f"sz_rows{t}") for t in range(PACK)]
        blocks = spans(Z_BLOCKS)
        last = len(blocks) - 1
        h_banks = []
        for b, (j0, width) in enumerate(blocks):
            cols = slice(j0, j0 + width)
            members = keep([P, PACK, width * MEMBERS], F32, f"members{b}")
            top = keep([P, PACK, width], F32, f"top{b}")
            z16 = keep([P, width * PACK], BF16, f"z16_{b}")
            entries = n1_sb[:, j0 * MEMBERS // 16 : (j0 + width) * MEMBERS // 16]

            def weigh(z_row, t):
                nc.vector.scalar_tensor_tensor(
                    z_row, top[:, t, :], neg_gn[:, t : t + 1], s_gn[:, t, cols], ALU.mult, ALU.add
                )

            if b < last:
                pairs = keep([P, PACK, width, 2], F32, f"pairs{b}")
                z32 = keep([P, PACK, width], F32, f"z32_{b}")
                for t in range(PACK):
                    nc.scalar.activation(members[:, t, :], s_rows[t][:].indirect(entries), ACT.Copy)
                    grouped = members[:, t, :].rearrange("p (j e) -> p j e", e=MEMBERS)
                    nc.vector.tensor_tensor(pairs[:, t, :, :], grouped[:, :, 0:2], grouped[:, :, 2:4], ALU.max)
                nc.vector.tensor_tensor(top[:], pairs[:, :, :, 0], pairs[:, :, :, 1], ALU.max)
                for t in range(PACK):
                    weigh(z32[:, t, :], t)
                interleave(z16, z32)
            else:
                for t in range(PACK):
                    nc.scalar.activation(members[:, t, :], s_rows[t][:].indirect(entries), ACT.Copy)
                    grouped = members[:, t, :].rearrange("p (j e) -> p j e", e=MEMBERS)
                    nc.vector.tensor_reduce(top[:, t, :], grouped, AX.X, ALU.max)
                    weigh(z16[:].rearrange("p (j t) -> p t j", t=PACK)[:, t, :], t)
            z_codes = keep([P, width], U32, f"z_codes{b}")
            z_plane = keep([P, width], U8, f"z_plane{b}")
            nc.vector.quantize_mx(out=z_codes[:].bitcast(FP8X4), scales=z_plane[:], in_=z16[:])

            def values(acc, t):
                nc.tensor.matmul_mx(
                    out=acc,
                    lhsT=w_codes[:, t * P : (t + 1) * P].bitcast(FP8X4),
                    lhsT_scale=w_plane[:, t * P : (t + 1) * P],
                    rhs=z_codes[:].bitcast(FP8X4),
                    rhs_scale=z_plane[:],
                    start=True,
                    stop=True,
                )

            if b < last:
                h_banks.append(ps.tile([P, PACK, width], F32, name=f"h_bank{b}", tag=f"bank{b}"))
                for t in range(PACK):
                    values(h_banks[b][:, t, :], t)
                if b != SCALAR_H_BLOCK:
                    nc.vector.tensor_copy(h_rows[:, :, cols], h_banks[b][:])
            else:
                h_last = [ps.tile([P, width], F32, name=f"h_last{t}", tag=f"bank{PACK + t}") for t in range(PACK)]
                for t in range(PACK):
                    values(h_last[t][:], t)

        j0, width = blocks[SCALAR_H_BLOCK]
        nc.scalar.activation(h_rows[:, :, j0 : j0 + width], h_banks[SCALAR_H_BLOCK][:], ACT.Copy)
        for cols in (slice(0, ABS_EARLY), slice(ABS_EARLY, blocks[last][0])):
            for t in range(PACK):
                nc.scalar.activation(sz_rows[t][:, cols], h_rows[:, t, cols], ACT.Abs)
        last_cols = slice(blocks[last][0], S)

        out_rows = out_0.rearrange("(p t) j -> p t j", t=PACK)
        out_words = as_words(out_1)
        y_plane = keep([P, S], U8, "y_plane")
        for b, (j0, width) in enumerate(spans(OUT_BLOCKS)):
            cols = slice(j0, j0 + width)
            entries = slice(j0 // 16, (j0 + width) // 16)
            h_other = keep([P, PACK, width], F32, f"h_other{b}")
            ea = keep([P, PACK, width], F32, f"ea{b}")

            def gate(t):
                nc.scalar.activation(
                    ea[:, t, :], sz_rows[t][:].indirect(n2_sb[:, entries]), ACT.Exp, scale=neg_tau[:, t : t + 1]
                )

            delta = keep([P, PACK, width], F32, f"delta{b}")
            if b == 0:
                for t in range(PACK):
                    nc.scalar.activation(sz_rows[t][:, last_cols], h_last[t][:], ACT.Abs)
                    nc.vector.tensor_copy(h_rows[:, t, last_cols], h_last[t][:])
                    gate(t)
                    nc.vector.tensor_copy(h_other[:, t, :], h_rows[:, t, :].indirect(n3_sb[:, entries]))
                    nc.gpsimd.tensor_tensor(delta[:, t, :], h_rows[:, t, cols], h_other[:, t, :], ALU.subtract)
            else:
                for t in range(PACK):
                    window = h_rows[:, t, :].indirect(n3_sb[:, entries])
                    if b == 1 and t < 2:
                        nc.vector.tensor_copy(h_other[:, t, :], window)
                    else:
                        nc.scalar.activation(h_other[:, t, :], window, ACT.Copy)
                for t in range(PACK):
                    gate(t)
            y32 = keep([P, PACK, width], F32, f"y32_{b}")
            if b > 0:
                nc.vector.tensor_tensor(delta[:], h_rows[:, :, cols], h_other[:], ALU.subtract)
            for rows in (slice(0, PACK),) if b == 1 else (slice(0, 2), slice(2, PACK)):
                nc.vector.tensor_tensor(y32[:, rows, :], delta[:, rows, :], ea[:, rows, :], ALU.mult)
            nc.sync.dma_start(out_rows[:, :, cols], y32[:])
            y16 = keep([P, width * PACK], BF16, f"y16_{b}")
            interleave(y16, y32)
            y_codes = keep([P, width], U32, f"y_codes{b}")
            nc.vector.quantize_mx(out=y_codes[:].bitcast(FP8X4), scales=y_plane[:, cols], in_=y16[:])
            nc.scalar.dma_start(out_words[:, cols], y_codes[:].bitcast(I32))
        scale_rows = out_2[0].bitcast(I32)
        for q in range(4):
            queue = nc.sync if q % 2 == 0 else nc.scalar
            queue.dma_start(scale_rows[4 * q : 4 * q + 4, :], y_plane[:].bitcast(I32)[32 * q : 32 * q + 4, :])
